import numpy as np
import ml_dtypes


def mxq(x, axis, fmt="e4m3"):
    dtype, down = {"e4m3": (ml_dtypes.float8_e4m3fn, 7), "e5m2": (ml_dtypes.float8_e5m2, 14)}[fmt]
    v = np.moveaxis(np.asarray(x, np.float32).astype(ml_dtypes.bfloat16).astype(np.float64), axis, -1)
    blocks = v.reshape(v.shape[:-1] + (-1, 32))
    amax = np.abs(blocks).max(-1, keepdims=True)
    byte = np.maximum(np.where(amax > 0, np.frexp(amax)[1] - 1 + 127, 0) - down, 1)
    scale = np.exp2(byte - 127.0)
    codes = (blocks / scale).astype(np.float32).astype(dtype).astype(np.float64)
    return np.moveaxis((codes * scale).reshape(v.shape), -1, axis)


WIDE = False


def mx_kscale(k):
    if not WIDE:
        return np.ones(k)
    levels = np.array([10, -10, 5, -5, 0])
    if k % 512:
        return np.exp2(np.random.permutation(np.resize(levels, k // 32))).repeat(32)
    a = np.empty((k // 512, 16))
    for p in range(k // 512):
        a[p, :8] = np.random.permutation(np.resize(levels, 8))
        for g in range(8):
            far = levels[np.abs(levels - a[p, g]) >= 10]
            a[p, g + 8] = far[np.random.randint(len(far))]
    return np.exp2(a.ravel()).repeat(32)


def f64(x):
    return np.asarray(x).astype(np.float64)


def striped(idx):
    return np.tile(np.asarray(idx).reshape(-1, 16).T, (8, 1)).astype(np.uint16)


def unstriped(offs):
    return offs[:16].T.reshape(-1).astype(np.int64)


E2M1 = np.array([0.0, 0.5, 1.0, 1.5, 2.0, 3.0, 4.0, 6.0, -0.0, -0.5, -1.0, -1.5, -2.0, -3.0, -4.0, -6.0])


def pack_weight(w, fmt):
    k, n = w.shape
    w = f64(np.asarray(w, np.float32).astype(ml_dtypes.bfloat16)).reshape(k // 32, 32, n)
    amax = np.abs(w).max(1)
    if fmt == "e4m3":
        byte = np.frexp(amax)[1] - 1 + 127 - 7
    else:
        mant, ex = np.frexp(amax / 6.0)
        byte = np.where(mant > 0.5, ex, ex - 1) + 127
    byte = np.clip(np.where(amax > 0, byte, 1), 1, 254)
    scaled = (w * np.exp2(127.0 - byte)[:, None, :]).reshape(k, n).astype(np.float32)
    by_word = np.ascontiguousarray(scaled.reshape(k // 512, 128, 4, n).transpose(0, 1, 3, 2))
    if fmt == "e4m3":
        words = by_word.astype(ml_dtypes.float8_e4m3fn).view(np.uint8)
    else:
        c = by_word.astype(ml_dtypes.float4_e2m1fn).view(np.uint8) & 0xF
        words = (c[..., 0::2] | (c[..., 1::2] << 4)).reshape(k // 512, 128, 2 * n)
    return np.ascontiguousarray(words), np.ascontiguousarray(byte.astype(np.uint8).reshape(k // 512, 16, n))


def unpack_weight(words, scales, fmt):
    g, _, n = scales.shape
    words = np.ascontiguousarray(words).reshape(g, 128, n, -1)
    if fmt == "e4m3":
        vals = words.view(ml_dtypes.float8_e4m3fn).astype(np.float64)
    else:
        nib = np.empty((g, 128, n, 4), np.uint8)
        nib[..., 0::2] = words & 0xF
        nib[..., 1::2] = words >> 4
        vals = E2M1[nib]
    vals = vals * np.repeat(np.exp2(scales.astype(np.float64) - 127.0), 8, axis=1)[..., None]
    return vals.transpose(0, 1, 3, 2).reshape(g * 512, n)


def sigmoid(v):
    return 1.0 / (1.0 + np.exp(-v))


def bf(x):
    return np.asarray(x, np.float32).astype(ml_dtypes.bfloat16)


def planes(Y):
    r, m = Y.shape
    b = f64(bf(Y)).reshape(r // 32, 32, m)
    amax = np.abs(b).max(1)
    byte = np.clip(np.where(amax > 0, np.frexp(amax)[1] - 1 + 127 - 7, 1), 1, 254)
    codes = (b * np.exp2(127.0 - byte)[:, None, :]).reshape(r, m).astype(np.float32).astype(ml_dtypes.float8_e4m3fn).view(np.uint8)
    words = codes.reshape(r // 512, 128, 4, m).transpose(0, 1, 3, 2)
    return np.ascontiguousarray(words), np.ascontiguousarray(byte.astype(np.uint8).reshape(r // 512, 16, m))


D, E, T, I, Q = 512, 512, 1024, 256, 512


def setup_inputs():
    n = np.random.standard_normal
    idx = np.random.permutation(T)[:I]
    idx2 = np.random.permutation(T)[:I]
    fd = mx_kscale(D)
    fq = mx_kscale(Q)
    keysp = pack_weight(n((D, T)) / fd[:, None], "e4m3")
    return {
        "query": (n((D, Q)) * 0.5 / np.sqrt(D) * fd[:, None]).astype(np.float32),
        "qs": (np.random.uniform(8.0, 32.0, (Q, 1)) * fq[:, None]).astype(np.float32),
        "grows": (n((Q, E)) / fq[:, None]).astype(np.float32),
        "vals": (n((E, T))).astype(np.float32),
        "keys_words": keysp[0],
        "keys_scales": keysp[1],
        "fr": (np.random.uniform(0.2, 0.8, (1, I))).astype(np.float32),
        "sg": (np.random.uniform(0.5, 2.0, (1, I))).astype(np.float32),
        "old": (0.5 * n((E, I))).astype(np.float32),
        "offs": striped(idx),
        "offs2": striped(idx2),
    }


def reference(query, qs, grows, vals, keys_words, keys_scales, fr, sg, old, offs, offs2):
    idx = unstriped(offs)
    idx2 = unstriped(offs2)
    keysu = unpack_weight(keys_words, keys_scales, "e4m3")
    queryq = mxq(f64(query), 0, "e4m3")
    keysidxg = keysu[:, idx]
    a = queryq.T @ keysidxg
    p = np.exp(a - np.max(a, axis=1, keepdims=True))
    w = p * f64(qs) / np.sum(p, axis=1, keepdims=True)
    growsq = mxq(f64(grows), 0, "e4m3")
    wq = mxq(w, 0, "e4m3")
    c0 = growsq.T @ wq
    x1 = f64(vals)[:, idx] * (1.0 - f64(fr)) + f64(vals)[:, idx2] * f64(fr)
    dx1 = c0 * sigmoid(x1) * (1.0 + x1 * (1.0 - sigmoid(x1)))
    y = dx1 * f64(sg) + f64(old)
    words, scales = planes(y)
    return y, words, scales

@@ -1,0 +1,261 @@
+from contextlib import ExitStack
+
+import concourse.mybir as mybir
+from concourse.masks import make_identity
+
+D, E, T, I, Q = 512, 512, 1024, 256, 512
+FLOPS = 2 * D * Q * I + 2 * Q * E * I
+
+F32 = mybir.dt.float32
+BF16 = mybir.dt.bfloat16
+I32 = mybir.dt.int32
+U32 = mybir.dt.uint32
+U16 = mybir.dt.uint16
+U8 = mybir.dt.uint8
+FP8X4 = mybir.dt.float8_e4m3fn_x4
+ALU = mybir.AluOpType
+ACT = mybir.ActivationFunctionType
+AX = mybir.AxisListType
+
+P = 128
+PACK = 4
+HALVES = I // P
+PAIRS = 2
+
+
+def deal_and_round(engine_copy, dealt, raw, lo, hi):
+    engine_copy(
+        out=dealt[:, :, lo:hi, :].rearrange("p r s j -> p s j r"),
+        in_=raw[:].rearrange("p j (s r) -> p s j r", r=PACK)[:, lo:hi, :, :],
+    )
+
+
+def tile_attend_bvbetween_d_pl_kernel(
+    tc, query, qs, grows, vals, keys_words, keys_scales, fr, sg, old, offs, offs2, out_0, out_1, out_2
+):
+    nc = tc.nc
+    with ExitStack() as ctx:
+        sb = ctx.enter_context(tc.tile_pool(name="sb", bufs=1))
+        ps = ctx.enter_context(tc.psum_pool(name="ps", bufs=1))
+
+        offs_sb = sb.tile([P, I // 16], U16, name="offs_sb")
+        offs2_sb = sb.tile([P, I // 16], U16, name="offs2_sb")
+        key_words = sb.tile([P, T], U32, name="key_words")
+        key_scales = sb.tile([P, T], U8, name="key_scales")
+        planes = [sb.tile([P, T], F32, name="plane%d" % t) for t in range(PACK)]
+        query_raw = sb.tile([P, PACK, Q], F32, name="query_raw")
+        grows_raw = sb.tile([P, PACK, E], F32, name="grows_raw")
+        old_sb = sb.tile([P, PACK, I], F32, name="old_sb")
+        fr_col = sb.tile([P, HALVES], F32, name="fr_col")
+        sg_col = sb.tile([P, HALVES], F32, name="sg_col")
+        qs_col = sb.tile([P, PACK], F32, name="qs_col")
+        ident = sb.tile([P, P], F32, name="ident")
+        warm_in = sb.tile([P, 1], F32, name="warm_in")
+        warm_out = sb.tile([P, 1], F32, name="warm_out")
+
+        nc.vector.memset(key_scales[:].bitcast(I32), 0)
+        nc.vector.memset(warm_in[:], 0.0)
+        nc.scalar.activation(out=warm_out[:], in_=warm_in[:], func=ACT.Exp)
+
+        vals_planes = vals.rearrange("(p t) n -> p t n", t=PACK)
+        nc.sync.dma_start(planes[0][:], vals_planes[:, 0, :])
+        nc.sync.dma_start(offs_sb[:], offs)
+        nc.sync.dma_start(offs2_sb[:], offs2)
+        for t in range(1, PACK):
+            nc.sync.dma_start(planes[t][:], vals_planes[:, t, :])
+        with nc.allow_non_contiguous_dma(reason="one slot to a partition"):
+            nc.sync.dma_start(fr_col[:], fr.rearrange("o (h k) -> k (o h)", h=HALVES))
+            nc.sync.dma_start(sg_col[:], sg.rearrange("o (h k) -> k (o h)", h=HALVES))
+        nc.sync.dma_start(query_raw[:], query.rearrange("(p j) q -> p j q", j=PACK))
+        nc.sync.dma_start(key_words[:].bitcast(I32), keys_words[0].rearrange("p n t -> p (n t)").bitcast(I32))
+        for quad in range(4):
+            nc.sync.dma_start(
+                key_scales[32 * quad : 32 * quad + 4, :].bitcast(I32),
+                keys_scales[0, 4 * quad : 4 * quad + 4, :].bitcast(I32),
+            )
+        nc.sync.dma_start(grows_raw[:], grows.rearrange("(p j) e -> p j e", j=PACK))
+        nc.sync.dma_start(qs_col[:], qs.rearrange("(s r) o -> s (r o)", r=PACK))
+        nc.sync.dma_start(old_sb[:], old.rearrange("(p t) i -> p t i", t=PACK))
+        make_identity(nc, ident[:])
+
+        rest_col = sb.tile([P, HALVES], F32, name="rest_col")
+        gain_col = sb.tile([P, HALVES], F32, name="gain_col")
+        nc.gpsimd.tensor_scalar(rest_col[:], fr_col[:], -1.0, 1.0, ALU.mult, ALU.add)
+        nc.gpsimd.tensor_scalar(gain_col[:], sg_col[:], -0.25, 0.0, ALU.mult, ALU.add)
+
+        slope = sb.tile([P, HALVES, E], F32, name="slope")
+        pair_w = E // PAIRS
+
+        def gather_plane(t, bank_a, bank_b):
+            tt = t % 2
+            for name, lst, bank in (("ga", offs_sb, bank_a), ("gb", offs2_sb, bank_b)):
+                got = sb.tile([P, I], F32, name="%s%d" % (name, t))
+                nc.vector.tensor_copy(got[:], planes[t][:].indirect(lst[:]))
+                for h in range(HALVES):
+                    nc.tensor.transpose(bank[:, h, tt * P : (tt + 1) * P], got[:, h * P : (h + 1) * P], ident[:])
+
+        def mix(u, bank_a, bank_b):
+            part = sb.tile([P, HALVES, pair_w], F32, name="part%d" % u)
+            x1 = sb.tile([P, HALVES, pair_w], F32, name="x1_%d" % u)
+            for h in range(HALVES):
+                nc.scalar.activation(out=part[:, h, :], in_=bank_a[:, h, :], func=ACT.Copy, scale=rest_col[:, h : h + 1])
+            for h in range(HALVES):
+                nc.vector.scalar_tensor_tensor(
+                    x1[:, h, :], bank_b[:, h, :], fr_col[:, h : h + 1], part[:, h, :], ALU.mult, ALU.add
+                )
+            return x1
+
+        def tanh_part(u, x1):
+            th = sb.tile([P, HALVES, pair_w], F32, name="th%d" % u)
+            lead = sb.tile([P, HALVES, pair_w], F32, name="lead%d" % u)
+            nc.scalar.activation(out=th[:], in_=x1[:], func=ACT.Tanh, scale=0.5)
+            for h in range(HALVES):
+                nc.scalar.activation(
+                    out=lead[:, h, :], in_=th[:, h, :], func=ACT.Identity,
+                    scale=gain_col[:, h : h + 1], bias=gain_col[:, h : h + 1],
+                )
+            return th, lead
+
+        def cross_part(u, x1, th):
+            cross = sb.tile([P, HALVES, pair_w], F32, name="cross%d" % u)
+            nc.vector.scalar_tensor_tensor(cross[:], th[:], -1.0, x1[:], ALU.add, ALU.mult)
+            return cross
+
+        def slope_part(u, cross, lead):
+            turned = sb.tile([P, HALVES, pair_w], F32, name="turned%d" % u)
+            nc.vector.scalar_tensor_tensor(turned[:], cross[:], -2.0, lead[:], ALU.add, ALU.mult)
+            back = ps.tile([P, HALVES, 2, P], F32, name="back%d" % u, tag="a%d" % u)
+            for h in range(HALVES):
+                for tt in range(2):
+                    nc.tensor.transpose(back[:, h, tt, :], turned[:, h, tt * P : (tt + 1) * P], ident[:])
+            nc.scalar.copy(
+                out=slope[:, :, u * pair_w : (u + 1) * pair_w], in_=back[:].rearrange("p h t i -> p h (t i)")
+            )
+
+        banks_a = [ps.tile([P, HALVES, pair_w], F32, name="bank_a%d" % u, tag="a%d" % u) for u in range(PAIRS)]
+        banks_b = [ps.tile([P, HALVES, pair_w], F32, name="bank_b%d" % u) for u in range(PAIRS)]
+
+        for t in range(PACK):
+            gather_plane(t, banks_a[t // 2], banks_b[t // 2])
+        x1s = [mix(u, banks_a[u], banks_b[u]) for u in range(PAIRS)]
+
+        query_bf = sb.tile([P, PACK, P, PACK], BF16, name="query_bf", align_bytes=64)
+        split = 40
+        deal_and_round(nc.scalar.copy, query_bf, query_raw, 0, split)
+        deal_and_round(nc.vector.tensor_copy, query_bf, query_raw, split, P)
+
+        key_codes = sb.tile([P, I], U32, name="key_codes", align_bytes=64)
+        key_bytes = sb.tile([P, I], U8, name="key_bytes", align_bytes=64)
+        nc.vector.tensor_copy(key_codes[:], key_words[:].indirect(offs_sb[:]))
+        nc.vector.tensor_copy(key_bytes[:], key_scales[:].indirect(offs_sb[:]))
+
+        query_codes = sb.tile([P, Q], U32, name="query_codes", align_bytes=64)
+        query_bytes = sb.tile([P, Q], U8, name="query_bytes", align_bytes=64)
+        nc.vector.quantize_mx(
+            out=query_codes[:].bitcast(FP8X4), scales=query_bytes[:],
+            in_=query_bf[:].rearrange("p r s j -> p (r s j)"),
+        )
+        scores = [ps.tile([P, 2, I], F32, name="scores%d" % b) for b in range(2)]
+        for r in range(PACK):
+            cols = slice(r * P, (r + 1) * P)
+            nc.tensor.matmul_mx(
+                out=scores[r // 2][:, r % 2, :],
+                lhsT=query_codes[:, cols].bitcast(FP8X4), lhsT_scale=query_bytes[:, cols],
+                rhs=key_codes[:].bitcast(FP8X4), rhs_scale=key_bytes[:],
+                start=True, stop=True,
+            )
+        parts = [tanh_part(u, x1s[u]) for u in range(PAIRS)]
+
+        neg_max = [sb.tile([P, 2], F32, name="neg_max%d" % b) for b in range(2)]
+        sums = sb.tile([P, PACK], F32, name="sums")
+        expo = sb.tile([P, PACK, I], F32, name="expo")
+        for b in range(2):
+            nc.vector.tensor_reduce(neg_max[b][:], scores[b][:], AX.X, ALU.max, negate=True)
+            for rr in range(2):
+                r = 2 * b + rr
+                nc.scalar.activation(
+                    out=expo[:, r, :], in_=scores[b][:, rr, :], func=ACT.Exp,
+                    bias=neg_max[b][:, rr : rr + 1], accum_out=sums[:, r : r + 1],
+                )
+
+        grows_bf = sb.tile([P, PACK, P, PACK], BF16, name="grows_bf", align_bytes=64)
+        deal_and_round(nc.scalar.copy, grows_bf, grows_raw, 0, P // 2)
+        deal_and_round(nc.scalar.copy, grows_bf, grows_raw, P // 2, P)
+
+        inv = sb.tile([P, PACK], F32, name="inv")
+        row_scale = sb.tile([P, PACK], F32, name="row_scale")
+        nc.vector.reciprocal(inv[:], sums[:])
+        nc.vector.tensor_tensor(row_scale[:], inv[:], qs_col[:], ALU.mult)
+        w_bf, w_codes, w_bytes = [], [], []
+        for h in range(HALVES):
+            wb = sb.tile([P, P, PACK], BF16, name="w_bf%d" % h, align_bytes=64)
+            nc.vector.tensor_tensor(
+                wb[:].rearrange("p (c i) r -> p c r i", i=4),
+                expo[:, :, h * P : (h + 1) * P].rearrange("p r (c i) -> p c r i", i=4),
+                row_scale[:].unsqueeze(1).unsqueeze(3).to_broadcast([P, P // 4, PACK, 4]),
+                ALU.mult,
+            )
+            w_bf.append(wb)
+        for h in range(HALVES):
+            wc = sb.tile([P, P], U32, name="w_codes%d" % h, align_bytes=64)
+            wsc = sb.tile([P, P], U8, name="w_bytes%d" % h, align_bytes=64)
+            nc.vector.quantize_mx(
+                out=wc[:].bitcast(FP8X4), scales=wsc[:], in_=w_bf[h][:].rearrange("p i r -> p (i r)")
+            )
+            w_codes.append(wc)
+            w_bytes.append(wsc)
+
+        grows_codes = sb.tile([P, E], U32, name="grows_codes", align_bytes=64)
+        grows_bytes = sb.tile([P, E], U8, name="grows_bytes", align_bytes=64)
+        nc.vector.quantize_mx(
+            out=grows_codes[:].bitcast(FP8X4), scales=grows_bytes[:],
+            in_=grows_bf[:].rearrange("p t m j -> p (t m j)"),
+        )
+        crosses = [cross_part(u, x1s[u], parts[u][0]) for u in range(PAIRS)]
+        for u in range(PAIRS):
+            slope_part(u, crosses[u], parts[u][1])
+
+        c0 = [ps.tile([P, PACK, P], F32, name="c0_%d" % h) for h in range(HALVES)]
+        for h in range(HALVES):
+            for t in range(PACK):
+                cols = slice(t * P, (t + 1) * P)
+                nc.tensor.matmul_mx(
+                    out=c0[h][:, t, :],
+                    lhsT=grows_codes[:, cols].bitcast(FP8X4), lhsT_scale=grows_bytes[:, cols],
+                    rhs=w_codes[h][:].bitcast(FP8X4), rhs_scale=w_bytes[h][:],
+                    start=True, stop=True,
+                )
+
+        y_codes = sb.tile([P, I], U32, name="y_codes", align_bytes=64)
+        y_bytes = sb.tile([P, I], U8, name="y_bytes", align_bytes=64)
+        out_rows = out_0.rearrange("(p t) i -> p t i", t=PACK)
+        dxs, y_bfs = [], []
+        for h in range(HALVES):
+            dx = sb.tile([P, E], F32, name="dx%d" % h)
+            nc.vector.tensor_tensor(dx[:], c0[h][:].rearrange("p t i -> p (t i)"), slope[:, h, :], ALU.mult)
+            dxs.append(dx)
+        for h in range(HALVES):
+            cols = slice(h * P, (h + 1) * P)
+            y = sb.tile([P, PACK, P], F32, name="y%d" % h)
+            nc.vector.tensor_tensor(y[:], dxs[h][:].rearrange("p (t i) -> p t i", t=PACK), old_sb[:, :, cols], ALU.add)
+            nc.sync.dma_start(out_rows[:, :, cols], y[:])
+            y_bf = sb.tile([P, P, PACK], BF16, name="y_bf%d" % h, align_bytes=64)
+            rounding = nc.scalar.copy if h == 0 else nc.vector.tensor_copy
+            rounding(
+                out=y_bf[:].rearrange("p (c i) t -> p c t i", i=4),
+                in_=y[:].rearrange("p t (c i) -> p c t i", i=4),
+            )
+            y_bfs.append(y_bf)
+        for h in range(HALVES):
+            cols = slice(h * P, (h + 1) * P)
+            nc.vector.quantize_mx(
+                out=y_codes[:, cols].bitcast(FP8X4), scales=y_bytes[:, cols],
+                in_=y_bfs[h][:].rearrange("p i t -> p (i t)"),
+            )
+        nc.sync.dma_start(out_1[0].rearrange("p n t -> p (n t)").bitcast(I32), y_codes[:].bitcast(I32))
+        for quad in range(4):
+            queue = nc.sync if quad % 2 == 0 else nc.scalar
+            queue.dma_start(
+                out_2[0, 4 * quad : 4 * quad + 4, :].bitcast(I32),
+                y_bytes[32 * quad : 32 * quad + 4, :].bitcast(I32),
+            )

@@ -21,12 +21,26 @@ P = 128
 PACK = 4
 HALVES = I // P
 PAIRS = 2
+PAIR_W = E // PAIRS
+TURNED, DIRECT = 0, 1
 
 
-def deal_and_round(engine_copy, dealt, raw, lo, hi):
-    engine_copy(
-        out=dealt[:, :, lo:hi, :].rearrange("p r s j -> p s j r"),
-        in_=raw[:].rearrange("p j (s r) -> p s j r", r=PACK)[:, lo:hi, :, :],
+def deal_and_round(copy, dealt, raw, part):
+    n = P // 2
+    copy(
+        out=dealt[:, :, part * n : (part + 1) * n, :].rearrange("p r s j -> p s j r"),
+        in_=raw[:].rearrange("p j (s r) -> p s j r", r=PACK),
+    )
+
+
+def quantize(nc, codes, scale_bytes, values):
+    nc.vector.quantize_mx(out=codes.bitcast(FP8X4), scales=scale_bytes, in_=values)
+
+
+def product(nc, out, lhs_codes, lhs_bytes, rhs_codes, rhs_bytes):
+    nc.tensor.matmul_mx(
+        out=out, lhsT=lhs_codes.bitcast(FP8X4), lhsT_scale=lhs_bytes,
+        rhs=rhs_codes.bitcast(FP8X4), rhs_scale=rhs_bytes, start=True, stop=True,
     )
 
 
@@ -43,8 +57,8 @@ def tile_attend_bvbetween_d_pl_kernel(
         key_words = sb.tile([P, T], U32, name="key_words")
         key_scales = sb.tile([P, T], U8, name="key_scales")
         planes = [sb.tile([P, T], F32, name="plane%d" % t) for t in range(PACK)]
-        query_raw = sb.tile([P, PACK, Q], F32, name="query_raw")
-        grows_raw = sb.tile([P, PACK, E], F32, name="grows_raw")
+        query_raw = [sb.tile([P, PACK, Q // 2], F32, name="query_raw%d" % k) for k in range(2)]
+        grows_raw = [sb.tile([P, PACK, E // 2], F32, name="grows_raw%d" % k) for k in range(2)]
         old_sb = sb.tile([P, PACK, I], F32, name="old_sb")
         fr_col = sb.tile([P, HALVES], F32, name="fr_col")
         sg_col = sb.tile([P, HALVES], F32, name="sg_col")
@@ -58,23 +72,28 @@ def tile_attend_bvbetween_d_pl_kernel(
         nc.scalar.activation(out=warm_out[:], in_=warm_in[:], func=ACT.Exp)
 
         vals_planes = vals.rearrange("(p t) n -> p t n", t=PACK)
+        query_rows = query.rearrange("(p j) q -> p j q", j=PACK)
+        grows_rows = grows.rearrange("(p j) e -> p j e", j=PACK)
         nc.sync.dma_start(planes[0][:], vals_planes[:, 0, :])
         nc.sync.dma_start(offs_sb[:], offs)
         nc.sync.dma_start(offs2_sb[:], offs2)
-        for t in range(1, PACK):
-            nc.sync.dma_start(planes[t][:], vals_planes[:, t, :])
         with nc.allow_non_contiguous_dma(reason="one slot to a partition"):
             nc.sync.dma_start(fr_col[:], fr.rearrange("o (h k) -> k (o h)", h=HALVES))
-            nc.sync.dma_start(sg_col[:], sg.rearrange("o (h k) -> k (o h)", h=HALVES))
-        nc.sync.dma_start(query_raw[:], query.rearrange("(p j) q -> p j q", j=PACK))
+        for t in range(1, PACK):
+            nc.sync.dma_start(planes[t][:], vals_planes[:, t, :])
+        nc.sync.dma_start(query_raw[0][:], query_rows[:, :, : Q // 2])
         nc.sync.dma_start(key_words[:].bitcast(I32), keys_words[0].rearrange("p n t -> p (n t)").bitcast(I32))
+        nc.sync.dma_start(query_raw[1][:], query_rows[:, :, Q // 2 :])
         for quad in range(4):
             nc.sync.dma_start(
                 key_scales[32 * quad : 32 * quad + 4, :].bitcast(I32),
                 keys_scales[0, 4 * quad : 4 * quad + 4, :].bitcast(I32),
             )
-        nc.sync.dma_start(grows_raw[:], grows.rearrange("(p j) e -> p j e", j=PACK))
+        with nc.allow_non_contiguous_dma(reason="one slot to a partition"):
+            nc.sync.dma_start(sg_col[:], sg.rearrange("o (h k) -> k (o h)", h=HALVES))
+        nc.sync.dma_start(grows_raw[0][:], grows_rows[:, :, : E // 2])
         nc.sync.dma_start(qs_col[:], qs.rearrange("(s r) o -> s (r o)", r=PACK))
+        nc.sync.dma_start(grows_raw[1][:], grows_rows[:, :, E // 2 :])
         nc.sync.dma_start(old_sb[:], old.rearrange("(p t) i -> p t i", t=PACK))
         make_identity(nc, ident[:])
 
@@ -83,175 +102,155 @@ def tile_attend_bvbetween_d_pl_kernel(
         nc.gpsimd.tensor_scalar(rest_col[:], fr_col[:], -1.0, 1.0, ALU.mult, ALU.add)
         nc.gpsimd.tensor_scalar(gain_col[:], sg_col[:], -0.25, 0.0, ALU.mult, ALU.add)
 
-        slope = sb.tile([P, HALVES, E], F32, name="slope")
-        pair_w = E // PAIRS
-
-        def gather_plane(t, bank_a, bank_b):
-            tt = t % 2
-            for name, lst, bank in (("ga", offs_sb, bank_a), ("gb", offs2_sb, bank_b)):
-                got = sb.tile([P, I], F32, name="%s%d" % (name, t))
-                nc.vector.tensor_copy(got[:], planes[t][:].indirect(lst[:]))
-                for h in range(HALVES):
-                    nc.tensor.transpose(bank[:, h, tt * P : (tt + 1) * P], got[:, h * P : (h + 1) * P], ident[:])
-
-        def mix(u, bank_a, bank_b):
-            part = sb.tile([P, HALVES, pair_w], F32, name="part%d" % u)
-            x1 = sb.tile([P, HALVES, pair_w], F32, name="x1_%d" % u)
-            for h in range(HALVES):
-                nc.scalar.activation(out=part[:, h, :], in_=bank_a[:, h, :], func=ACT.Copy, scale=rest_col[:, h : h + 1])
-            for h in range(HALVES):
-                nc.vector.scalar_tensor_tensor(
-                    x1[:, h, :], bank_b[:, h, :], fr_col[:, h : h + 1], part[:, h, :], ALU.mult, ALU.add
-                )
-            return x1
-
-        def tanh_part(u, x1):
-            th = sb.tile([P, HALVES, pair_w], F32, name="th%d" % u)
-            lead = sb.tile([P, HALVES, pair_w], F32, name="lead%d" % u)
-            nc.scalar.activation(out=th[:], in_=x1[:], func=ACT.Tanh, scale=0.5)
-            for h in range(HALVES):
-                nc.scalar.activation(
-                    out=lead[:, h, :], in_=th[:, h, :], func=ACT.Identity,
-                    scale=gain_col[:, h : h + 1], bias=gain_col[:, h : h + 1],
-                )
-            return th, lead
-
-        def cross_part(u, x1, th):
-            cross = sb.tile([P, HALVES, pair_w], F32, name="cross%d" % u)
-            nc.vector.scalar_tensor_tensor(cross[:], th[:], -1.0, x1[:], ALU.add, ALU.mult)
-            return cross
-
-        def slope_part(u, cross, lead):
-            turned = sb.tile([P, HALVES, pair_w], F32, name="turned%d" % u)
-            nc.vector.scalar_tensor_tensor(turned[:], cross[:], -2.0, lead[:], ALU.add, ALU.mult)
-            back = ps.tile([P, HALVES, 2, P], F32, name="back%d" % u, tag="a%d" % u)
-            for h in range(HALVES):
-                for tt in range(2):
-                    nc.tensor.transpose(back[:, h, tt, :], turned[:, h, tt * P : (tt + 1) * P], ident[:])
-            nc.scalar.copy(
-                out=slope[:, :, u * pair_w : (u + 1) * pair_w], in_=back[:].rearrange("p h t i -> p h (t i)")
-            )
-
-        banks_a = [ps.tile([P, HALVES, pair_w], F32, name="bank_a%d" % u, tag="a%d" % u) for u in range(PAIRS)]
-        banks_b = [ps.tile([P, HALVES, pair_w], F32, name="bank_b%d" % u) for u in range(PAIRS)]
-
-        for t in range(PACK):
-            gather_plane(t, banks_a[t // 2], banks_b[t // 2])
-        x1s = [mix(u, banks_a[u], banks_b[u]) for u in range(PAIRS)]
-
         query_bf = sb.tile([P, PACK, P, PACK], BF16, name="query_bf", align_bytes=64)
-        split = 40
-        deal_and_round(nc.scalar.copy, query_bf, query_raw, 0, split)
-        deal_and_round(nc.vector.tensor_copy, query_bf, query_raw, split, P)
+        deal_and_round(nc.scalar.copy, query_bf, query_raw[0], 0)
+        deal_and_round(nc.vector.tensor_copy, query_bf, query_raw[1], 1)
 
         key_codes = sb.tile([P, I], U32, name="key_codes", align_bytes=64)
         key_bytes = sb.tile([P, I], U8, name="key_bytes", align_bytes=64)
         nc.vector.tensor_copy(key_codes[:], key_words[:].indirect(offs_sb[:]))
         nc.vector.tensor_copy(key_bytes[:], key_scales[:].indirect(offs_sb[:]))
 
-        query_codes = sb.tile([P, Q], U32, name="query_codes", align_bytes=64)
-        query_bytes = sb.tile([P, Q], U8, name="query_bytes", align_bytes=64)
-        nc.vector.quantize_mx(
-            out=query_codes[:].bitcast(FP8X4), scales=query_bytes[:],
-            in_=query_bf[:].rearrange("p r s j -> p (r s j)"),
-        )
-        scores = [ps.tile([P, 2, I], F32, name="scores%d" % b) for b in range(2)]
-        for r in range(PACK):
-            cols = slice(r * P, (r + 1) * P)
-            nc.tensor.matmul_mx(
-                out=scores[r // 2][:, r % 2, :],
-                lhsT=query_codes[:, cols].bitcast(FP8X4), lhsT_scale=query_bytes[:, cols],
-                rhs=key_codes[:].bitcast(FP8X4), rhs_scale=key_bytes[:],
-                start=True, stop=True,
+        query_codes = [sb.tile([P, 2 * P], U32, name="query_codes%d" % k, align_bytes=64) for k in range(2)]
+        query_bytes = [sb.tile([P, 2 * P], U8, name="query_bytes%d" % k, align_bytes=64) for k in range(2)]
+        for k in range(2):
+            quantize(
+                nc, query_codes[k][:], query_bytes[k][:],
+                query_bf[:, 2 * k : 2 * k + 2, :, :].rearrange("p r s j -> p (r s j)"),
             )
-        parts = [tanh_part(u, x1s[u]) for u in range(PAIRS)]
+        scores = [ps.tile([P, I], F32, name="scores%d" % r, tag="mx%d" % r) for r in range(PACK)]
+        for r in range(PACK):
+            cols = slice(r % 2 * P, (r % 2 + 1) * P)
+            product(nc, scores[r][:], query_codes[r // 2][:, cols], query_bytes[r // 2][:, cols], key_codes[:], key_bytes[:])
 
-        neg_max = [sb.tile([P, 2], F32, name="neg_max%d" % b) for b in range(2)]
         sums = sb.tile([P, PACK], F32, name="sums")
         expo = sb.tile([P, PACK, I], F32, name="expo")
-        for b in range(2):
-            nc.vector.tensor_reduce(neg_max[b][:], scores[b][:], AX.X, ALU.max, negate=True)
-            for rr in range(2):
-                r = 2 * b + rr
-                nc.scalar.activation(
-                    out=expo[:, r, :], in_=scores[b][:, rr, :], func=ACT.Exp,
-                    bias=neg_max[b][:, rr : rr + 1], accum_out=sums[:, r : r + 1],
-                )
-
-        grows_bf = sb.tile([P, PACK, P, PACK], BF16, name="grows_bf", align_bytes=64)
-        deal_and_round(nc.scalar.copy, grows_bf, grows_raw, 0, P // 2)
-        deal_and_round(nc.scalar.copy, grows_bf, grows_raw, P // 2, P)
-
+        for r in range(PACK):
+            neg_max = sb.tile([P, 1], F32, name="neg_max%d" % r)
+            nc.vector.tensor_reduce(neg_max[:], scores[r][:], AX.X, ALU.max, negate=True)
+            nc.scalar.activation(
+                out=expo[:, r, :], in_=scores[r][:], func=ACT.Exp, bias=neg_max[:], accum_out=sums[:, r : r + 1]
+            )
         inv = sb.tile([P, PACK], F32, name="inv")
         row_scale = sb.tile([P, PACK], F32, name="row_scale")
         nc.vector.reciprocal(inv[:], sums[:])
         nc.vector.tensor_tensor(row_scale[:], inv[:], qs_col[:], ALU.mult)
-        w_bf, w_codes, w_bytes = [], [], []
+        w_bf = [sb.tile([P, P, PACK], BF16, name="w_bf%d" % h, align_bytes=64) for h in range(HALVES)]
+        w_codes = [sb.tile([P, P], U32, name="w_codes%d" % h, align_bytes=64) for h in range(HALVES)]
+        w_bytes = [sb.tile([P, P], U8, name="w_bytes%d" % h, align_bytes=64) for h in range(HALVES)]
         for h in range(HALVES):
-            wb = sb.tile([P, P, PACK], BF16, name="w_bf%d" % h, align_bytes=64)
             nc.vector.tensor_tensor(
-                wb[:].rearrange("p (c i) r -> p c r i", i=4),
+                w_bf[h][:].rearrange("p (c i) r -> p c r i", i=4),
                 expo[:, :, h * P : (h + 1) * P].rearrange("p r (c i) -> p c r i", i=4),
                 row_scale[:].unsqueeze(1).unsqueeze(3).to_broadcast([P, P // 4, PACK, 4]),
                 ALU.mult,
             )
-            w_bf.append(wb)
         for h in range(HALVES):
-            wc = sb.tile([P, P], U32, name="w_codes%d" % h, align_bytes=64)
-            wsc = sb.tile([P, P], U8, name="w_bytes%d" % h, align_bytes=64)
-            nc.vector.quantize_mx(
-                out=wc[:].bitcast(FP8X4), scales=wsc[:], in_=w_bf[h][:].rearrange("p i r -> p (i r)")
-            )
-            w_codes.append(wc)
-            w_bytes.append(wsc)
+            quantize(nc, w_codes[h][:], w_bytes[h][:], w_bf[h][:].rearrange("p i r -> p (i r)"))
 
+        banks_a = [ps.tile([P, HALVES, PAIR_W], F32, name="bank_a%d" % u, tag="a%d" % u) for u in range(PAIRS)]
+        banks_b = [ps.tile([P, HALVES, PAIR_W], F32, name="bank_b%d" % u, tag="b%d" % u) for u in range(PAIRS)]
+        for t in range(PACK):
+            for name, lst, bank in (("first", offs_sb, banks_a[t // 2]), ("second", offs2_sb, banks_b[t // 2])):
+                got = sb.tile([P, I], F32, name="%s%d" % (name, t))
+                nc.vector.tensor_copy(got[:], planes[t][:].indirect(lst[:]))
+                for h in range(HALVES):
+                    nc.tensor.transpose(
+                        bank[:, h, t % 2 * P : (t % 2 + 1) * P], got[:, h * P : (h + 1) * P], ident[:]
+                    )
+
+        order = (DIRECT, TURNED)
+        part = [sb.tile([P, E], F32, name="part%d" % h) for h in range(HALVES)]
+        x1 = [sb.tile([P, E], F32, name="x1_%d" % h) for h in range(HALVES)]
+        for u in range(PAIRS):
+            cols = slice(u * PAIR_W, (u + 1) * PAIR_W)
+            for h in order:
+                nc.scalar.activation(
+                    out=part[h][:, cols], in_=banks_a[u][:, h, :], func=ACT.Copy, scale=rest_col[:, h : h + 1]
+                )
+            for h in order:
+                nc.vector.scalar_tensor_tensor(
+                    x1[h][:, cols], banks_b[u][:, h, :], fr_col[:, h : h + 1], part[h][:, cols], ALU.mult, ALU.add
+                )
+
+        th = [sb.tile([P, E], F32, name="th%d" % h) for h in range(HALVES)]
+        lead = [sb.tile([P, E], F32, name="lead%d" % h) for h in range(HALVES)]
+        cross = [sb.tile([P, E], F32, name="cross%d" % h) for h in range(HALVES)]
+        slope_t = [sb.tile([P, E], F32, name="slope_t%d" % h) for h in range(HALVES)]
+
+        def make_lead(h):
+            nc.scalar.activation(
+                out=lead[h][:], in_=th[h][:], func=ACT.Identity,
+                scale=gain_col[:, h : h + 1], bias=gain_col[:, h : h + 1],
+            )
+
+        def make_slope(h):
+            nc.vector.scalar_tensor_tensor(slope_t[h][:], cross[h][:], -2.0, lead[h][:], ALU.add, ALU.mult)
+
+        for h in order:
+            nc.scalar.activation(out=th[h][:], in_=x1[h][:], func=ACT.Tanh, scale=0.5)
+        make_lead(DIRECT)
+        for h in order:
+            nc.vector.scalar_tensor_tensor(cross[h][:], th[h][:], -1.0, x1[h][:], ALU.add, ALU.mult)
+        make_slope(DIRECT)
+        slope_ps = ps.tile([P, PACK, P], F32, name="slope_ps", tag="a1")
+        for t in range(PACK):
+            nc.tensor.transpose(slope_ps[:, t, :], slope_t[DIRECT][:, t * P : (t + 1) * P], ident[:])
+
+        grows_bf = sb.tile([P, PACK, P, PACK], BF16, name="grows_bf", align_bytes=64)
+        for k in range(2):
+            deal_and_round(nc.scalar.copy, grows_bf, grows_raw[k], k)
         grows_codes = sb.tile([P, E], U32, name="grows_codes", align_bytes=64)
         grows_bytes = sb.tile([P, E], U8, name="grows_bytes", align_bytes=64)
-        nc.vector.quantize_mx(
-            out=grows_codes[:].bitcast(FP8X4), scales=grows_bytes[:],
-            in_=grows_bf[:].rearrange("p t m j -> p (t m j)"),
-        )
-        crosses = [cross_part(u, x1s[u], parts[u][0]) for u in range(PAIRS)]
-        for u in range(PAIRS):
-            slope_part(u, crosses[u], parts[u][1])
+        quantize(nc, grows_codes[:], grows_bytes[:], grows_bf[:].rearrange("p t m j -> p (t m j)"))
+        c0_turned = ps.tile([P, E], F32, name="c0_turned", tag="mx0")
+        product(nc, c0_turned[:], w_codes[TURNED][:], w_bytes[TURNED][:], grows_codes[:], grows_bytes[:])
+        c0_direct = ps.tile([P, PACK, P], F32, name="c0_direct", tag="mx1")
+        for t in range(PACK):
+            cols = slice(t * P, (t + 1) * P)
+            product(nc, c0_direct[:, t, :], grows_codes[:, cols], grows_bytes[:, cols], w_codes[DIRECT][:], w_bytes[DIRECT][:])
 
-        c0 = [ps.tile([P, PACK, P], F32, name="c0_%d" % h) for h in range(HALVES)]
-        for h in range(HALVES):
-            for t in range(PACK):
-                cols = slice(t * P, (t + 1) * P)
-                nc.tensor.matmul_mx(
-                    out=c0[h][:, t, :],
-                    lhsT=grows_codes[:, cols].bitcast(FP8X4), lhsT_scale=grows_bytes[:, cols],
-                    rhs=w_codes[h][:].bitcast(FP8X4), rhs_scale=w_bytes[h][:],
-                    start=True, stop=True,
-                )
+        slots = [slice(h * P, (h + 1) * P) for h in range(HALVES)]
+        old_ps = ps.tile([P, PACK, P], F32, name="old_ps", tag="a0")
+        for t in range(PACK):
+            nc.tensor.transpose(old_ps[:, t, :], old_sb[:, t, slots[TURNED]], ident[:])
+        old_t = sb.tile([P, PACK, P], F32, name="old_t")
+        nc.scalar.copy(out=old_t[:], in_=old_ps[:])
+        y_ps = ps.tile([P, PACK, P], F32, name="y_ps", tag="b0")
+        for t in range(PACK):
+            nc.tensor.matmul(y_ps[:, t, :], old_t[:, t, :], ident[:], start=(t == 0), stop=False, is_transpose=True)
+
+        slope = sb.tile([P, PACK, P], F32, name="slope")
+        nc.scalar.copy(out=slope[:], in_=slope_ps[:])
+        make_lead(TURNED)
+        make_slope(TURNED)
+
+        out_rows = out_0.rearrange("(p t) i -> p t i", t=PACK)
+        y = [sb.tile([P, PACK, P], F32, name="y%d" % h) for h in range(HALVES)]
+        y_bf = [sb.tile([P, P, PACK], BF16, name="y_bf%d" % h, align_bytes=64) for h in range(HALVES)]
+        dx_turned = sb.tile([P, E], F32, name="dx_turned")
+        nc.vector.tensor_tensor(dx_turned[:], c0_turned[:], slope_t[TURNED][:], ALU.mult)
+        for t in range(PACK):
+            nc.tensor.matmul(
+                y_ps[:, t, :], dx_turned[:, t * P : (t + 1) * P], ident[:],
+                start=False, stop=(t == PACK - 1), is_transpose=True,
+            )
+        dx_direct = sb.tile([P, PACK, P], F32, name="dx_direct")
+        nc.vector.tensor_tensor(dx_direct[:], c0_direct[:], slope[:], ALU.mult)
+        nc.vector.tensor_tensor(y[DIRECT][:], dx_direct[:], old_sb[:, :, slots[DIRECT]], ALU.add)
+        nc.sync.dma_start(out_rows[:, :, slots[DIRECT]], y[DIRECT][:])
+        nc.vector.tensor_copy(
+            out=y_bf[DIRECT][:].rearrange("p (c i) t -> p c t i", i=4),
+            in_=y[DIRECT][:].rearrange("p t (c i) -> p c t i", i=4),
+        )
+        nc.scalar.copy(out=y_bf[TURNED][:], in_=y_ps[:].rearrange("p t i -> p i t"))
+        nc.scalar.copy(out=y[TURNED][:], in_=y_ps[:])
+        nc.scalar.dma_start(out_rows[:, :, slots[TURNED]], y[TURNED][:])
 
         y_codes = sb.tile([P, I], U32, name="y_codes", align_bytes=64)
         y_bytes = sb.tile([P, I], U8, name="y_bytes", align_bytes=64)
-        out_rows = out_0.rearrange("(p t) i -> p t i", t=PACK)
-        dxs, y_bfs = [], []
-        for h in range(HALVES):
-            dx = sb.tile([P, E], F32, name="dx%d" % h)
-            nc.vector.tensor_tensor(dx[:], c0[h][:].rearrange("p t i -> p (t i)"), slope[:, h, :], ALU.mult)
-            dxs.append(dx)
-        for h in range(HALVES):
-            cols = slice(h * P, (h + 1) * P)
-            y = sb.tile([P, PACK, P], F32, name="y%d" % h)
-            nc.vector.tensor_tensor(y[:], dxs[h][:].rearrange("p (t i) -> p t i", t=PACK), old_sb[:, :, cols], ALU.add)
-            nc.sync.dma_start(out_rows[:, :, cols], y[:])
-            y_bf = sb.tile([P, P, PACK], BF16, name="y_bf%d" % h, align_bytes=64)
-            rounding = nc.scalar.copy if h == 0 else nc.vector.tensor_copy
-            rounding(
-                out=y_bf[:].rearrange("p (c i) t -> p c t i", i=4),
-                in_=y[:].rearrange("p t (c i) -> p c t i", i=4),
-            )
-            y_bfs.append(y_bf)
-        for h in range(HALVES):
-            cols = slice(h * P, (h + 1) * P)
-            nc.vector.quantize_mx(
-                out=y_codes[:, cols].bitcast(FP8X4), scales=y_bytes[:, cols],
-                in_=y_bfs[h][:].rearrange("p i t -> p (i t)"),
-            )
+        for h in order:
+            quantize(nc, y_codes[:, slots[h]], y_bytes[:, slots[h]], y_bf[h][:].rearrange("p i t -> p (i t)"))
         nc.sync.dma_start(out_1[0].rearrange("p n t -> p (n t)").bitcast(I32), y_codes[:].bitcast(I32))
         for quad in range(4):
             queue = nc.sync if quad % 2 == 0 else nc.scalar

@@ -25,12 +25,8 @@ PAIR_W = E // PAIRS
 TURNED, DIRECT = 0, 1
 
 
-def deal_and_round(copy, dealt, raw, part):
-    n = P // 2
-    copy(
-        out=dealt[:, :, part * n : (part + 1) * n, :].rearrange("p r s j -> p s j r"),
-        in_=raw[:].rearrange("p j (s r) -> p s j r", r=PACK),
-    )
+def deal_and_round(copy, dealt, raw):
+    copy(out=dealt.rearrange("p r s j -> p s j r"), in_=raw.rearrange("p j (s r) -> p s j r", r=PACK))
 
 
 def quantize(nc, codes, scale_bytes, values):
@@ -57,16 +53,18 @@ def tile_attend_bvbetween_d_pl_kernel(
         key_words = sb.tile([P, T], U32, name="key_words")
         key_scales = sb.tile([P, T], U8, name="key_scales")
         planes = [sb.tile([P, T], F32, name="plane%d" % t) for t in range(PACK)]
-        query_raw = [sb.tile([P, PACK, Q // 2], F32, name="query_raw%d" % k) for k in range(2)]
+        query_raw = sb.tile([P, PACK, Q], F32, name="query_raw")
         grows_raw = [sb.tile([P, PACK, E // 2], F32, name="grows_raw%d" % k) for k in range(2)]
         old_sb = sb.tile([P, PACK, I], F32, name="old_sb")
-        fr_col = sb.tile([P, HALVES], F32, name="fr_col")
-        sg_col = sb.tile([P, HALVES], F32, name="sg_col")
+        slot_rows = sb.tile([P, P], F32, name="slot_rows")
         qs_col = sb.tile([P, PACK], F32, name="qs_col")
         ident = sb.tile([P, P], F32, name="ident")
         warm_in = sb.tile([P, 1], F32, name="warm_in")
         warm_out = sb.tile([P, 1], F32, name="warm_out")
 
+        nc.vector.memset(slot_rows[:], 0.0)
+        nc.scalar.dma_start(slot_rows[0:HALVES, :], fr.rearrange("o (h k) -> (o h) k", h=HALVES))
+        nc.scalar.dma_start(slot_rows[HALVES : 2 * HALVES, :], sg.rearrange("o (h k) -> (o h) k", h=HALVES))
         nc.vector.memset(key_scales[:].bitcast(I32), 0)
         nc.vector.memset(warm_in[:], 0.0)
         nc.scalar.activation(out=warm_out[:], in_=warm_in[:], func=ACT.Exp)
@@ -77,34 +75,34 @@ def tile_attend_bvbetween_d_pl_kernel(
         nc.sync.dma_start(planes[0][:], vals_planes[:, 0, :])
         nc.sync.dma_start(offs_sb[:], offs)
         nc.sync.dma_start(offs2_sb[:], offs2)
-        with nc.allow_non_contiguous_dma(reason="one slot to a partition"):
-            nc.sync.dma_start(fr_col[:], fr.rearrange("o (h k) -> k (o h)", h=HALVES))
         for t in range(1, PACK):
             nc.sync.dma_start(planes[t][:], vals_planes[:, t, :])
-        nc.sync.dma_start(query_raw[0][:], query_rows[:, :, : Q // 2])
+        nc.sync.dma_start(query_raw[:], query_rows)
         nc.sync.dma_start(key_words[:].bitcast(I32), keys_words[0].rearrange("p n t -> p (n t)").bitcast(I32))
-        nc.sync.dma_start(query_raw[1][:], query_rows[:, :, Q // 2 :])
         for quad in range(4):
             nc.sync.dma_start(
                 key_scales[32 * quad : 32 * quad + 4, :].bitcast(I32),
                 keys_scales[0, 4 * quad : 4 * quad + 4, :].bitcast(I32),
             )
-        with nc.allow_non_contiguous_dma(reason="one slot to a partition"):
-            nc.sync.dma_start(sg_col[:], sg.rearrange("o (h k) -> k (o h)", h=HALVES))
         nc.sync.dma_start(grows_raw[0][:], grows_rows[:, :, : E // 2])
-        nc.sync.dma_start(qs_col[:], qs.rearrange("(s r) o -> s (r o)", r=PACK))
         nc.sync.dma_start(grows_raw[1][:], grows_rows[:, :, E // 2 :])
+        nc.sync.dma_start(qs_col[:], qs.rearrange("(s r) o -> s (r o)", r=PACK))
         nc.sync.dma_start(old_sb[:], old.rearrange("(p t) i -> p t i", t=PACK))
         make_identity(nc, ident[:])
 
         rest_col = sb.tile([P, HALVES], F32, name="rest_col")
         gain_col = sb.tile([P, HALVES], F32, name="gain_col")
-        nc.gpsimd.tensor_scalar(rest_col[:], fr_col[:], -1.0, 1.0, ALU.mult, ALU.add)
-        nc.gpsimd.tensor_scalar(gain_col[:], sg_col[:], -0.25, 0.0, ALU.mult, ALU.add)
+        fr_col = sb.tile([P, HALVES], F32, name="fr_col")
+        slot_cols = ps.tile([P, P], F32, name="slot_cols", tag="mx3")
+        nc.tensor.transpose(slot_cols[:], slot_rows[:], ident[:])
+        nc.scalar.activation(out=rest_col[:], in_=slot_cols[:, 0:HALVES], func=ACT.Copy, scale=-1.0, bias=1.0)
+        nc.scalar.copy(out=fr_col[:], in_=slot_cols[:, 0:HALVES])
+        nc.scalar.activation(out=gain_col[:], in_=slot_cols[:, HALVES : 2 * HALVES], func=ACT.Copy, scale=-0.25)
 
         query_bf = sb.tile([P, PACK, P, PACK], BF16, name="query_bf", align_bytes=64)
-        deal_and_round(nc.scalar.copy, query_bf, query_raw[0], 0)
-        deal_and_round(nc.vector.tensor_copy, query_bf, query_raw[1], 1)
+        split = 40
+        deal_and_round(nc.scalar.copy, query_bf[:, :, :split, :], query_raw[:, :, : PACK * split])
+        deal_and_round(nc.vector.tensor_copy, query_bf[:, :, split:, :], query_raw[:, :, PACK * split :])
 
         key_codes = sb.tile([P, I], U32, name="key_codes", align_bytes=64)
         key_bytes = sb.tile([P, I], U8, name="key_bytes", align_bytes=64)
@@ -199,7 +197,7 @@ def tile_attend_bvbetween_d_pl_kernel(
 
         grows_bf = sb.tile([P, PACK, P, PACK], BF16, name="grows_bf", align_bytes=64)
         for k in range(2):
-            deal_and_round(nc.scalar.copy, grows_bf, grows_raw[k], k)
+            deal_and_round(nc.scalar.copy, grows_bf[:, :, k * P // 2 : (k + 1) * P // 2, :], grows_raw[k][:])
         grows_codes = sb.tile([P, E], U32, name="grows_codes", align_bytes=64)
         grows_bytes = sb.tile([P, E], U8, name="grows_bytes", align_bytes=64)
         quantize(nc, grows_codes[:], grows_bytes[:], grows_bf[:].rearrange("p t m j -> p (t m j)"))

@@ -62,10 +62,10 @@ def tile_attend_bvbetween_d_pl_kernel(
         warm_in = sb.tile([P, 1], F32, name="warm_in")
         warm_out = sb.tile([P, 1], F32, name="warm_out")
 
-        nc.vector.memset(slot_rows[:], 0.0)
+        nc.vector.memset(key_scales[:].bitcast(I32), 0)
+        nc.gpsimd.memset(slot_rows[:], 0.0)
         nc.scalar.dma_start(slot_rows[0:HALVES, :], fr.rearrange("o (h k) -> (o h) k", h=HALVES))
         nc.scalar.dma_start(slot_rows[HALVES : 2 * HALVES, :], sg.rearrange("o (h k) -> (o h) k", h=HALVES))
-        nc.vector.memset(key_scales[:].bitcast(I32), 0)
         nc.vector.memset(warm_in[:], 0.0)
         nc.scalar.activation(out=warm_out[:], in_=warm_in[:], func=ACT.Exp)
 
@@ -77,13 +77,13 @@ def tile_attend_bvbetween_d_pl_kernel(
         nc.sync.dma_start(offs2_sb[:], offs2)
         for t in range(1, PACK):
             nc.sync.dma_start(planes[t][:], vals_planes[:, t, :])
-        nc.sync.dma_start(query_raw[:], query_rows)
-        nc.sync.dma_start(key_words[:].bitcast(I32), keys_words[0].rearrange("p n t -> p (n t)").bitcast(I32))
         for quad in range(4):
             nc.sync.dma_start(
                 key_scales[32 * quad : 32 * quad + 4, :].bitcast(I32),
                 keys_scales[0, 4 * quad : 4 * quad + 4, :].bitcast(I32),
             )
+        nc.sync.dma_start(query_raw[:], query_rows)
+        nc.sync.dma_start(key_words[:].bitcast(I32), keys_words[0].rearrange("p n t -> p (n t)").bitcast(I32))
         nc.sync.dma_start(grows_raw[0][:], grows_rows[:, :, : E // 2])
         nc.sync.dma_start(grows_raw[1][:], grows_rows[:, :, E // 2 :])
         nc.sync.dma_start(qs_col[:], qs.rearrange("(s r) o -> s (r o)", r=PACK))

@@ -22,7 +22,10 @@ PACK = 4
 HALVES = I // P
 PAIRS = 2
 PAIR_W = E // PAIRS
+LINE = 4
+QUADS = 4
 TURNED, DIRECT = 0, 1
+SCALAR_GROUPS = 24
 
 
 def deal_and_round(copy, dealt, raw):
@@ -59,15 +62,11 @@ def tile_attend_bvbetween_d_pl_kernel(
         slot_rows = sb.tile([P, P], F32, name="slot_rows")
         qs_col = sb.tile([P, PACK], F32, name="qs_col")
         ident = sb.tile([P, P], F32, name="ident")
-        warm_in = sb.tile([P, 1], F32, name="warm_in")
-        warm_out = sb.tile([P, 1], F32, name="warm_out")
 
         nc.vector.memset(key_scales[:].bitcast(I32), 0)
         nc.gpsimd.memset(slot_rows[:], 0.0)
         nc.scalar.dma_start(slot_rows[0:HALVES, :], fr.rearrange("o (h k) -> (o h) k", h=HALVES))
         nc.scalar.dma_start(slot_rows[HALVES : 2 * HALVES, :], sg.rearrange("o (h k) -> (o h) k", h=HALVES))
-        nc.vector.memset(warm_in[:], 0.0)
-        nc.scalar.activation(out=warm_out[:], in_=warm_in[:], func=ACT.Exp)
 
         vals_planes = vals.rearrange("(p t) n -> p t n", t=PACK)
         query_rows = query.rearrange("(p j) q -> p j q", j=PACK)
@@ -77,7 +76,7 @@ def tile_attend_bvbetween_d_pl_kernel(
         nc.sync.dma_start(offs2_sb[:], offs2)
         for t in range(1, PACK):
             nc.sync.dma_start(planes[t][:], vals_planes[:, t, :])
-        for quad in range(4):
+        for quad in range(QUADS):
             nc.sync.dma_start(
                 key_scales[32 * quad : 32 * quad + 4, :].bitcast(I32),
                 keys_scales[0, 4 * quad : 4 * quad + 4, :].bitcast(I32),
@@ -100,9 +99,8 @@ def tile_attend_bvbetween_d_pl_kernel(
         nc.scalar.activation(out=gain_col[:], in_=slot_cols[:, HALVES : 2 * HALVES], func=ACT.Copy, scale=-0.25)
 
         query_bf = sb.tile([P, PACK, P, PACK], BF16, name="query_bf", align_bytes=64)
-        split = 40
-        deal_and_round(nc.scalar.copy, query_bf[:, :, :split, :], query_raw[:, :, : PACK * split])
-        deal_and_round(nc.vector.tensor_copy, query_bf[:, :, split:, :], query_raw[:, :, PACK * split :])
+        deal_and_round(nc.scalar.copy, query_bf[:, :, :SCALAR_GROUPS, :], query_raw[:, :, : PACK * SCALAR_GROUPS])
+        deal_and_round(nc.vector.tensor_copy, query_bf[:, :, SCALAR_GROUPS:, :], query_raw[:, :, PACK * SCALAR_GROUPS :])
 
         key_codes = sb.tile([P, I], U32, name="key_codes", align_bytes=64)
         key_bytes = sb.tile([P, I], U8, name="key_bytes", align_bytes=64)
@@ -138,9 +136,9 @@ def tile_attend_bvbetween_d_pl_kernel(
         w_bytes = [sb.tile([P, P], U8, name="w_bytes%d" % h, align_bytes=64) for h in range(HALVES)]
         for h in range(HALVES):
             nc.vector.tensor_tensor(
-                w_bf[h][:].rearrange("p (c i) r -> p c r i", i=4),
-                expo[:, :, h * P : (h + 1) * P].rearrange("p r (c i) -> p c r i", i=4),
-                row_scale[:].unsqueeze(1).unsqueeze(3).to_broadcast([P, P // 4, PACK, 4]),
+                w_bf[h][:].rearrange("p (c i) r -> p c r i", i=LINE),
+                expo[:, :, h * P : (h + 1) * P].rearrange("p r (c i) -> p c r i", i=LINE),
+                row_scale[:].unsqueeze(1).unsqueeze(3).to_broadcast([P, P // LINE, PACK, LINE]),
                 ALU.mult,
             )
         for h in range(HALVES):
@@ -238,8 +236,8 @@ def tile_attend_bvbetween_d_pl_kernel(
         nc.vector.tensor_tensor(y[DIRECT][:], dx_direct[:], old_sb[:, :, slots[DIRECT]], ALU.add)
         nc.sync.dma_start(out_rows[:, :, slots[DIRECT]], y[DIRECT][:])
         nc.vector.tensor_copy(
-            out=y_bf[DIRECT][:].rearrange("p (c i) t -> p c t i", i=4),
-            in_=y[DIRECT][:].rearrange("p t (c i) -> p c t i", i=4),
+            out=y_bf[DIRECT][:].rearrange("p (c i) t -> p c t i", i=LINE),
+            in_=y[DIRECT][:].rearrange("p t (c i) -> p c t i", i=LINE),
         )
         nc.scalar.copy(out=y_bf[TURNED][:], in_=y_ps[:].rearrange("p t i -> p i t"))
         nc.scalar.copy(out=y[TURNED][:], in_=y_ps[:])
@@ -250,7 +248,7 @@ def tile_attend_bvbetween_d_pl_kernel(
         for h in order:
             quantize(nc, y_codes[:, slots[h]], y_bytes[:, slots[h]], y_bf[h][:].rearrange("p i t -> p (i t)"))
         nc.sync.dma_start(out_1[0].rearrange("p n t -> p (n t)").bitcast(I32), y_codes[:].bitcast(I32))
-        for quad in range(4):
+        for quad in range(QUADS):
             queue = nc.sync if quad % 2 == 0 else nc.scalar
             queue.dma_start(
                 out_2[0, 4 * quad : 4 * quad + 4, :].bitcast(I32),

from contextlib import ExitStack

import concourse.mybir as mybir
from concourse.masks import make_identity

D, E, T, I, Q = 512, 512, 1024, 256, 512
FLOPS = 2 * D * Q * I + 2 * Q * E * I

F32 = mybir.dt.float32
BF16 = mybir.dt.bfloat16
I32 = mybir.dt.int32
U32 = mybir.dt.uint32
U16 = mybir.dt.uint16
U8 = mybir.dt.uint8
FP8X4 = mybir.dt.float8_e4m3fn_x4
ALU = mybir.AluOpType
ACT = mybir.ActivationFunctionType
AX = mybir.AxisListType

P = 128
PACK = 4
HALVES = I // P
PAIRS = 2
PAIR_W = E // PAIRS
LINE = 4
QUADS = 4
TURNED, DIRECT = 0, 1
SCALAR_GROUPS = 24


def deal_and_round(copy, dealt, raw):
    copy(out=dealt.rearrange("p r s j -> p s j r"), in_=raw.rearrange("p j (s r) -> p s j r", r=PACK))


def quantize(nc, codes, scale_bytes, values):
    nc.vector.quantize_mx(out=codes.bitcast(FP8X4), scales=scale_bytes, in_=values)


def product(nc, out, lhs_codes, lhs_bytes, rhs_codes, rhs_bytes):
    nc.tensor.matmul_mx(
        out=out, lhsT=lhs_codes.bitcast(FP8X4), lhsT_scale=lhs_bytes,
        rhs=rhs_codes.bitcast(FP8X4), rhs_scale=rhs_bytes, start=True, stop=True,
    )


def tile_attend_bvbetween_d_pl_kernel(
    tc, query, qs, grows, vals, keys_words, keys_scales, fr, sg, old, offs, offs2, out_0, out_1, out_2
):
    nc = tc.nc
    with ExitStack() as ctx:
        sb = ctx.enter_context(tc.tile_pool(name="sb", bufs=1))
        ps = ctx.enter_context(tc.psum_pool(name="ps", bufs=1))

        offs_sb = sb.tile([P, I // 16], U16, name="offs_sb")
        offs2_sb = sb.tile([P, I // 16], U16, name="offs2_sb")
        key_words = sb.tile([P, T], U32, name="key_words")
        key_scales = sb.tile([P, T], U8, name="key_scales")
        planes = [sb.tile([P, T], F32, name="plane%d" % t) for t in range(PACK)]
        query_raw = sb.tile([P, PACK, Q], F32, name="query_raw")
        grows_raw = [sb.tile([P, PACK, E // 2], F32, name="grows_raw%d" % k) for k in range(2)]
        old_sb = sb.tile([P, PACK, I], F32, name="old_sb")
        slot_rows = sb.tile([P, P], F32, name="slot_rows")
        qs_col = sb.tile([P, PACK], F32, name="qs_col")
        ident = sb.tile([P, P], F32, name="ident")

        nc.vector.memset(key_scales[:].bitcast(I32), 0)
        nc.gpsimd.memset(slot_rows[:], 0.0)
        nc.scalar.dma_start(slot_rows[0:HALVES, :], fr.rearrange("o (h k) -> (o h) k", h=HALVES))
        nc.scalar.dma_start(slot_rows[HALVES : 2 * HALVES, :], sg.rearrange("o (h k) -> (o h) k", h=HALVES))

        vals_planes = vals.rearrange("(p t) n -> p t n", t=PACK)
        query_rows = query.rearrange("(p j) q -> p j q", j=PACK)
        grows_rows = grows.rearrange("(p j) e -> p j e", j=PACK)
        nc.sync.dma_start(planes[0][:], vals_planes[:, 0, :])
        nc.sync.dma_start(offs_sb[:], offs)
        nc.sync.dma_start(offs2_sb[:], offs2)
        for t in range(1, PACK):
            nc.sync.dma_start(planes[t][:], vals_planes[:, t, :])
        for quad in range(QUADS):
            nc.sync.dma_start(
                key_scales[32 * quad : 32 * quad + 4, :].bitcast(I32),
                keys_scales[0, 4 * quad : 4 * quad + 4, :].bitcast(I32),
            )
        nc.sync.dma_start(query_raw[:], query_rows)
        nc.sync.dma_start(key_words[:].bitcast(I32), keys_words[0].rearrange("p n t -> p (n t)").bitcast(I32))
        nc.sync.dma_start(grows_raw[0][:], grows_rows[:, :, : E // 2])
        nc.sync.dma_start(grows_raw[1][:], grows_rows[:, :, E // 2 :])
        nc.sync.dma_start(qs_col[:], qs.rearrange("(s r) o -> s (r o)", r=PACK))
        nc.sync.dma_start(old_sb[:], old.rearrange("(p t) i -> p t i", t=PACK))
        make_identity(nc, ident[:])

        rest_col = sb.tile([P, HALVES], F32, name="rest_col")
        gain_col = sb.tile([P, HALVES], F32, name="gain_col")
        fr_col = sb.tile([P, HALVES], F32, name="fr_col")
        slot_cols = ps.tile([P, P], F32, name="slot_cols", tag="mx3")
        nc.tensor.transpose(slot_cols[:], slot_rows[:], ident[:])
        nc.scalar.activation(out=rest_col[:], in_=slot_cols[:, 0:HALVES], func=ACT.Copy, scale=-1.0, bias=1.0)
        nc.scalar.copy(out=fr_col[:], in_=slot_cols[:, 0:HALVES])
        nc.scalar.activation(out=gain_col[:], in_=slot_cols[:, HALVES : 2 * HALVES], func=ACT.Copy, scale=-0.25)

        query_bf = sb.tile([P, PACK, P, PACK], BF16, name="query_bf", align_bytes=64)
        deal_and_round(nc.scalar.copy, query_bf[:, :, :SCALAR_GROUPS, :], query_raw[:, :, : PACK * SCALAR_GROUPS])
        deal_and_round(nc.vector.tensor_copy, query_bf[:, :, SCALAR_GROUPS:, :], query_raw[:, :, PACK * SCALAR_GROUPS :])

        key_codes = sb.tile([P, I], U32, name="key_codes", align_bytes=64)
        key_bytes = sb.tile([P, I], U8, name="key_bytes", align_bytes=64)
        nc.vector.tensor_copy(key_codes[:], key_words[:].indirect(offs_sb[:]))
        nc.vector.tensor_copy(key_bytes[:], key_scales[:].indirect(offs_sb[:]))

        query_codes = [sb.tile([P, 2 * P], U32, name="query_codes%d" % k, align_bytes=64) for k in range(2)]
        query_bytes = [sb.tile([P, 2 * P], U8, name="query_bytes%d" % k, align_bytes=64) for k in range(2)]
        for k in range(2):
            quantize(
                nc, query_codes[k][:], query_bytes[k][:],
                query_bf[:, 2 * k : 2 * k + 2, :, :].rearrange("p r s j -> p (r s j)"),
            )
        scores = [ps.tile([P, I], F32, name="scores%d" % r, tag="mx%d" % r) for r in range(PACK)]
        for r in range(PACK):
            cols = slice(r % 2 * P, (r % 2 + 1) * P)
            product(nc, scores[r][:], query_codes[r // 2][:, cols], query_bytes[r // 2][:, cols], key_codes[:], key_bytes[:])

        sums = sb.tile([P, PACK], F32, name="sums")
        expo = sb.tile([P, PACK, I], F32, name="expo")
        for r in range(PACK):
            neg_max = sb.tile([P, 1], F32, name="neg_max%d" % r)
            nc.vector.tensor_reduce(neg_max[:], scores[r][:], AX.X, ALU.max, negate=True)
            nc.scalar.activation(
                out=expo[:, r, :], in_=scores[r][:], func=ACT.Exp, bias=neg_max[:], accum_out=sums[:, r : r + 1]
            )
        inv = sb.tile([P, PACK], F32, name="inv")
        row_scale = sb.tile([P, PACK], F32, name="row_scale")
        nc.vector.reciprocal(inv[:], sums[:])
        nc.vector.tensor_tensor(row_scale[:], inv[:], qs_col[:], ALU.mult)
        w_bf = [sb.tile([P, P, PACK], BF16, name="w_bf%d" % h, align_bytes=64) for h in range(HALVES)]
        w_codes = [sb.tile([P, P], U32, name="w_codes%d" % h, align_bytes=64) for h in range(HALVES)]
        w_bytes = [sb.tile([P, P], U8, name="w_bytes%d" % h, align_bytes=64) for h in range(HALVES)]
        for h in range(HALVES):
            nc.vector.tensor_tensor(
                w_bf[h][:].rearrange("p (c i) r -> p c r i", i=LINE),
                expo[:, :, h * P : (h + 1) * P].rearrange("p r (c i) -> p c r i", i=LINE),
                row_scale[:].unsqueeze(1).unsqueeze(3).to_broadcast([P, P // LINE, PACK, LINE]),
                ALU.mult,
            )
        for h in range(HALVES):
            quantize(nc, w_codes[h][:], w_bytes[h][:], w_bf[h][:].rearrange("p i r -> p (i r)"))

        banks_a = [ps.tile([P, HALVES, PAIR_W], F32, name="bank_a%d" % u, tag="a%d" % u) for u in range(PAIRS)]
        banks_b = [ps.tile([P, HALVES, PAIR_W], F32, name="bank_b%d" % u, tag="b%d" % u) for u in range(PAIRS)]
        for t in range(PACK):
            for name, lst, bank in (("first", offs_sb, banks_a[t // 2]), ("second", offs2_sb, banks_b[t // 2])):
                got = sb.tile([P, I], F32, name="%s%d" % (name, t))
                nc.vector.tensor_copy(got[:], planes[t][:].indirect(lst[:]))
                for h in range(HALVES):
                    nc.tensor.transpose(
                        bank[:, h, t % 2 * P : (t % 2 + 1) * P], got[:, h * P : (h + 1) * P], ident[:]
                    )

        order = (DIRECT, TURNED)
        part = [sb.tile([P, E], F32, name="part%d" % h) for h in range(HALVES)]
        x1 = [sb.tile([P, E], F32, name="x1_%d" % h) for h in range(HALVES)]
        for u in range(PAIRS):
            cols = slice(u * PAIR_W, (u + 1) * PAIR_W)
            for h in order:
                nc.scalar.activation(
                    out=part[h][:, cols], in_=banks_a[u][:, h, :], func=ACT.Copy, scale=rest_col[:, h : h + 1]
                )
            for h in order:
                nc.vector.scalar_tensor_tensor(
                    x1[h][:, cols], banks_b[u][:, h, :], fr_col[:, h : h + 1], part[h][:, cols], ALU.mult, ALU.add
                )

        th = [sb.tile([P, E], F32, name="th%d" % h) for h in range(HALVES)]
        lead = [sb.tile([P, E], F32, name="lead%d" % h) for h in range(HALVES)]
        cross = [sb.tile([P, E], F32, name="cross%d" % h) for h in range(HALVES)]
        slope_t = [sb.tile([P, E], F32, name="slope_t%d" % h) for h in range(HALVES)]

        def make_lead(h):
            nc.scalar.activation(
                out=lead[h][:], in_=th[h][:], func=ACT.Identity,
                scale=gain_col[:, h : h + 1], bias=gain_col[:, h : h + 1],
            )

        def make_slope(h):
            nc.vector.scalar_tensor_tensor(slope_t[h][:], cross[h][:], -2.0, lead[h][:], ALU.add, ALU.mult)

        for h in order:
            nc.scalar.activation(out=th[h][:], in_=x1[h][:], func=ACT.Tanh, scale=0.5)
        make_lead(DIRECT)
        for h in order:
            nc.vector.scalar_tensor_tensor(cross[h][:], th[h][:], -1.0, x1[h][:], ALU.add, ALU.mult)
        make_slope(DIRECT)
        slope_ps = ps.tile([P, PACK, P], F32, name="slope_ps", tag="a1")
        for t in range(PACK):
            nc.tensor.transpose(slope_ps[:, t, :], slope_t[DIRECT][:, t * P : (t + 1) * P], ident[:])

        grows_bf = sb.tile([P, PACK, P, PACK], BF16, name="grows_bf", align_bytes=64)
        for k in range(2):
            deal_and_round(nc.scalar.copy, grows_bf[:, :, k * P // 2 : (k + 1) * P // 2, :], grows_raw[k][:])
        grows_codes = sb.tile([P, E], U32, name="grows_codes", align_bytes=64)
        grows_bytes = sb.tile([P, E], U8, name="grows_bytes", align_bytes=64)
        quantize(nc, grows_codes[:], grows_bytes[:], grows_bf[:].rearrange("p t m j -> p (t m j)"))
        c0_turned = ps.tile([P, E], F32, name="c0_turned", tag="mx0")
        product(nc, c0_turned[:], w_codes[TURNED][:], w_bytes[TURNED][:], grows_codes[:], grows_bytes[:])
        c0_direct = ps.tile([P, PACK, P], F32, name="c0_direct", tag="mx1")
        for t in range(PACK):
            cols = slice(t * P, (t + 1) * P)
            product(nc, c0_direct[:, t, :], grows_codes[:, cols], grows_bytes[:, cols], w_codes[DIRECT][:], w_bytes[DIRECT][:])

        slots = [slice(h * P, (h + 1) * P) for h in range(HALVES)]
        old_ps = ps.tile([P, PACK, P], F32, name="old_ps", tag="a0")
        for t in range(PACK):
            nc.tensor.transpose(old_ps[:, t, :], old_sb[:, t, slots[TURNED]], ident[:])
        old_t = sb.tile([P, PACK, P], F32, name="old_t")
        nc.scalar.copy(out=old_t[:], in_=old_ps[:])
        y_ps = ps.tile([P, PACK, P], F32, name="y_ps", tag="b0")
        for t in range(PACK):
            nc.tensor.matmul(y_ps[:, t, :], old_t[:, t, :], ident[:], start=(t == 0), stop=False, is_transpose=True)

        slope = sb.tile([P, PACK, P], F32, name="slope")
        nc.scalar.copy(out=slope[:], in_=slope_ps[:])
        make_lead(TURNED)
        make_slope(TURNED)

        out_rows = out_0.rearrange("(p t) i -> p t i", t=PACK)
        y = [sb.tile([P, PACK, P], F32, name="y%d" % h) for h in range(HALVES)]
        y_bf = [sb.tile([P, P, PACK], BF16, name="y_bf%d" % h, align_bytes=64) for h in range(HALVES)]
        dx_turned = sb.tile([P, E], F32, name="dx_turned")
        nc.vector.tensor_tensor(dx_turned[:], c0_turned[:], slope_t[TURNED][:], ALU.mult)
        for t in range(PACK):
            nc.tensor.matmul(
                y_ps[:, t, :], dx_turned[:, t * P : (t + 1) * P], ident[:],
                start=False, stop=(t == PACK - 1), is_transpose=True,
            )
        dx_direct = sb.tile([P, PACK, P], F32, name="dx_direct")
        nc.vector.tensor_tensor(dx_direct[:], c0_direct[:], slope[:], ALU.mult)
        nc.vector.tensor_tensor(y[DIRECT][:], dx_direct[:], old_sb[:, :, slots[DIRECT]], ALU.add)
        nc.sync.dma_start(out_rows[:, :, slots[DIRECT]], y[DIRECT][:])
        nc.vector.tensor_copy(
            out=y_bf[DIRECT][:].rearrange("p (c i) t -> p c t i", i=LINE),
            in_=y[DIRECT][:].rearrange("p t (c i) -> p c t i", i=LINE),
        )
        nc.scalar.copy(out=y_bf[TURNED][:], in_=y_ps[:].rearrange("p t i -> p i t"))
        nc.scalar.copy(out=y[TURNED][:], in_=y_ps[:])
        nc.scalar.dma_start(out_rows[:, :, slots[TURNED]], y[TURNED][:])

        y_codes = sb.tile([P, I], U32, name="y_codes", align_bytes=64)
        y_bytes = sb.tile([P, I], U8, name="y_bytes", align_bytes=64)
        for h in order:
            quantize(nc, y_codes[:, slots[h]], y_bytes[:, slots[h]], y_bf[h][:].rearrange("p i t -> p (i t)"))
        nc.sync.dma_start(out_1[0].rearrange("p n t -> p (n t)").bitcast(I32), y_codes[:].bitcast(I32))
        for quad in range(QUADS):
            queue = nc.sync if quad % 2 == 0 else nc.scalar
            queue.dma_start(
                out_2[0, 4 * quad : 4 * quad + 4, :].bitcast(I32),
                y_bytes[32 * quad : 32 * quad + 4, :].bitcast(I32),
            )
